import numpy as np, ml_dtypes
CORES = [242,247,114,119]
N = 4
import mx_ref
NC = 256
EPS = 0.001
BF = ml_dtypes.bfloat16
def setup_inputs(rng):
    def f(*shape):
        return mx_ref.flush((rng.standard_normal(shape, dtype=np.float32) * np.exp2(rng.integers(-2, 3, shape[:-1] + (1,)))).astype(BF))
    return {"x": f(N, 128, 512), "w": f(N, 128, 4 * NC)}
def setup_inputs_blocks(rng):
    d = setup_inputs(rng)
    for k in ("x", "w"): d[k] = mx_ref.spread(d[k], rng, 4)
    return d
def setup_inputs_wide(rng):
    d = setup_inputs(rng)
    for k in ("x", "w"): d[k] = mx_ref.flush((d[k].astype(np.float32) * np.exp2(rng.integers(-6, 7, (N, 1, 1))).astype(np.float32)).astype(BF))
    return d
def setup_inputs_tokens(rng):
    d = setup_inputs(rng); v = d["x"].astype(np.float32).reshape(N, 128, -1, 4)
    d["x"] = mx_ref.flush((v * np.exp2(rng.integers(-6, 7, (N, 1, v.shape[2], 1))).astype(np.float32)).reshape(d["x"].shape).astype(BF))
    return d
def setup_inputs_faint(rng):
    d = setup_inputs(rng); d["x"] = mx_ref.flush((d["x"].astype(np.float32) * np.float32(2.0 ** -12)).astype(BF))
    return d
def reference(x, w):
    W = [mx_ref.quantize(w[r]) for r in range(N)]
    y = np.zeros((N, 128, N * NC), np.float32)
    for j in range(N):
        X = mx_ref.quantize(x[j])
        Z = [mx_ref.matmul(X, W[r]) for r in range(N)]
        ms = sum((z.astype(np.float64) ** 2).sum(axis=1, keepdims=True) for z in Z) / (N * NC)
        for r in range(N):
            y[r][:, NC * j:NC * j + NC] = (Z[r] / np.sqrt(ms + EPS)).astype(np.float32)
    return {"y": y}

@@ -1,0 +1,197 @@
+from concourse.bass import DstId, RemoteDMATransfer
+from concourse.mybir import dt, AluOpType, ActivationFunctionType
+
+N, NC, TK, EPS = 4, 256, 128, 0.001
+K = 20
+NCHAIN = 32
+
+SCRATCH = {
+    "xb": ("sbuf", [128, 4 * TK], "bfloat16"),
+    "wb": ("sbuf", [128, 4 * NC], "bfloat16"),
+    "xq": ("sbuf", [128, N * TK], "float8_e4m3fn_x4"),
+    "xs": ("sbuf", [128, N * TK], "uint8"),
+    "wq": ("sbuf", [128, 2 * NC], "float8_e4m3fn_x4"),
+    "ws": ("sbuf", [128, 2 * NC], "uint8"),
+    "z": ("psum", [128, 512 * 6], "float32"),
+    "sq": ("sbuf", [128, 6 * NC], "float32"),
+    "le": ("sbuf", [128, 4 * N], "float32"),
+    "ll": ("sbuf", [128, 4 * N], "float32"),
+    "tmp": ("sbuf", [128, 4 * 28], "float32"),
+    "ysb": ("sbuf", [128, N * NC], "float32"),
+}
+SEMAPHORES = (["ldx", "ldw", "qx", "qw", "wa", "sqE", "sqL", "sqP", "eaP", "eaR", "snt", "yE", "yL", "stE", "stL"]
+              + ["xa%d" % j for j in range(N)] + ["la%d" % j for j in range(N)] + ["mm%d" % j for j in range(6)]
+              + ["c%d" % j for j in range(NCHAIN)])
+
+
+def _plan(topo, cores, s):
+    c = cores[s]
+    here = [j for j in range(N) if topo.host(cores[j]) == topo.host(c) and topo.chip(cores[j]) == topo.chip(c)]
+    far = [j for j in range(N) if j not in here]
+    far_o = sorted(far, key=lambda j: (topo.die(cores[j]) != topo.die(c), j))
+    p = [j for j in here if j != s][0]
+
+    def bits(m):
+        return [e for e in range(m.bit_length()) if (m >> e) & 1]
+    off = bits(topo.mask(c, cores[far[0]]))
+    on = [e for e in bits(topo.mask(c, cores[p])) if e not in off]
+    h = len(off) // 2
+    return here, far, far_o, p, {far_o[0]: off[:h], far_o[1]: off[h:], p: on}
+
+
+def rank_program(g, core, T, topo):
+    r = T.rank_of(core)
+    if r is None:
+        return
+    cores = T.cores
+    V, S, PE, SY = g.vector, g.scalar, g.tensor, g.sync
+    A, F = AluOpType, ActivationFunctionType
+    here, far, far_o, p, eng = _plan(topo, cores, r)
+
+    def nin(s):
+        return len(_plan(topo, cores, s)[4][r])
+    sent = [0]
+    nsem = [0]
+
+    def new_sem():
+        nsem[0] += 1
+        return T.sem["c%d" % (nsem[0] - 1)]
+
+    def send(src, dst, dests):
+        trs = []
+        for d, sem in dests:
+            rid, pid = topo.addr(cores[d], core)
+            trs.append(RemoteDMATransfer(dst_ids=[DstId(rid=rid, pnc=pid)], dma_engine_mask=sum(1 << e for e in eng[d]),
+                                         remote_sem=sem, src=src, dst=dst))
+            sent[0] += len(eng[d])
+        g.remote_dma_fused(trs, local_sem=T.sem.snt)
+
+    def xcol(j):
+        return slice(TK * j, TK * j + TK)
+
+    def le(j):
+        return T.le[:, 4 * j:4 * j + 2]
+
+    def ll(j):
+        return T.ll[:, 4 * j:4 * j + 2]
+    nslot = [0]
+
+    def slot():
+        nslot[0] += 1
+        return T.tmp[:, 4 * (nslot[0] - 1):4 * (nslot[0] - 1) + 2]
+
+    SY.dma_start(T.xb[:], T.x[:]).then_inc(T.sem.ldx, 16)
+    SY.dma_start(T.wb[:], T.w[:]).then_inc(T.sem.ldw, 16)
+    V.wait_ge(T.sem.ldx, 16)
+    V.quantize_mx(T.xq[:, xcol(r)], T.xs[:, xcol(r)], T.xb[:]).then_inc(T.sem.qx, 1)
+    V.wait_ge(T.sem.ldw, 16)
+    V.quantize_mx(T.wq[:, 0:NC], T.ws[:, 0:NC], T.wb[:]).then_inc(T.sem.qw, 1)
+
+    others = [far_o[0], far_o[1], p]
+    xa = T.sem["xa%d" % r]
+    g.wait_ge(T.sem.qx, 1)
+    cx = T.xq[:, xcol(r)].bitcast(dt.uint8)
+    send(cx, cx, [(d, xa) for d in others])
+    send(T.xs[:, xcol(r)], T.xs[:, xcol(r)], [(d, xa) for d in others])
+    g.wait_ge(T.sem.qw, 1)
+    send(T.wq[:, 0:NC].bitcast(dt.uint8), T.wq[:, NC:2 * NC].bitcast(dt.uint8), [(p, T.sem.wa)])
+    send(T.ws[:, 0:NC], T.ws[:, NC:2 * NC], [(p, T.sem.wa)])
+    g.wait_ge(T.sem.sqE, 2)
+    send(le(r), le(r), [(far_o[0], T.sem.eaR), (far_o[1], T.sem.eaR), (p, T.sem.eaP)])
+    g.wait_ge(T.sem.sqL, 2)
+    send(ll(r), ll(r), [(d, T.sem["la%d" % r]) for d in far_o])
+    g.wait_ge(T.sem.snt, sent[0])
+
+    def mm(j, wlo, bank):
+        PE.matmul_mx(T.z[:, 512 * bank:512 * bank + NC], T.xq[:, xcol(j)], T.xs[:, xcol(j)],
+                     T.wq[:, wlo:wlo + NC], T.ws[:, wlo:wlo + NC], True, True).then_inc(T.sem["mm%d" % bank], 1)
+    PE.wait_ge(T.sem.qx, 1)
+    PE.wait_ge(T.sem.qw, 1)
+    mm(r, 0, r)
+    for j in [p] + far_o:
+        PE.wait_ge(T.sem["xa%d" % j], 2 * nin(j))
+        mm(j, 0, j)
+    PE.wait_ge(T.sem.wa, 2 * nin(p))
+    for i, j in enumerate(far_o):
+        mm(j, NC, N + i)
+
+    def square(bank, acc, sem):
+        S.wait_ge(T.sem["mm%d" % bank], 1)
+        S.activation(T.sq[:, NC * bank:NC * bank + NC], T.z[:, 512 * bank:512 * bank + NC], F.Square,
+                     scale=2.0 ** -K, accum_out=acc).then_inc(sem, 1)
+    for j in [r, p]:
+        c = 4 * r + here.index(j)
+        square(j, T.le[:, c:c + 1], T.sem.sqE)
+    for j in far_o:
+        c = 4 * r + far.index(j)
+        square(j, T.ll[:, c:c + 1], T.sem.sqL)
+    for i, j in enumerate(far_o):
+        c = 4 * p + far.index(j)
+        square(N + i, T.ll[:, c:c + 1], T.sem.sqP)
+
+    def add(a, b):
+        o, s = slot(), new_sem()
+        V.tensor_tensor(o, a, b, A.add).then_inc(s, 1)
+        return o, s
+
+    def finish(tot, s_tot, blocks, ysem, between=None):
+        q, v, u, a, b, t, rr = [slot() for _ in range(7)]
+        sq_, sv, su, sa, sb, st, sr = [new_sem() for _ in range(7)]
+        S.wait_ge(s_tot, 1)
+        S.activation(q, tot, F.Sqrt, bias=EPS * 2.0 ** (-2 * K), scale=1.0 / (N * NC)).then_inc(sq_, 1)
+        V.wait_ge(s_tot, 1)
+        V.tensor_scalar(v, tot, 2.0 ** K / (N * NC), EPS * 2.0 ** -K, A.mult, A.add).then_inc(sv, 1)
+        V.wait_ge(sv, 1)
+        V.reciprocal(u, v).then_inc(su, 1)
+        res = between() if between else None
+        V.wait_ge(su, 1)
+        V.wait_ge(sq_, 1)
+        V.tensor_tensor(a, q, u, A.mult).then_inc(sa, 1)
+        V.wait_ge(sa, 1)
+        V.tensor_tensor(b, a, q, A.mult).then_inc(sb, 1)
+        V.wait_ge(sb, 1)
+        V.tensor_scalar(t, b, -0.5 * 2.0 ** K, 1.5, A.mult, A.add).then_inc(st, 1)
+        V.wait_ge(st, 1)
+        V.tensor_tensor(rr, a, t, A.mult).then_inc(sr, 1)
+        V.wait_ge(sr, 1)
+        S.wait_ge(sr, 1)
+        j0, j1 = blocks
+        V.tensor_scalar(T.ysb[:, NC * j0:NC * j0 + NC], T.z[:, 512 * j0:512 * j0 + NC], rr[:, 0:1], None,
+                        A.mult).then_inc(ysem, 1)
+        S.activation(T.ysb[:, NC * j1:NC * j1 + NC], T.z[:, 512 * j1:512 * j1 + NC], F.Copy,
+                     scale=rr[:, 1:2]).then_inc(ysem, 1)
+        return res
+
+    V.wait_ge(T.sem.eaR, nin(far[0]) + nin(far[1]))
+    e2, s2 = add(le(far[0]), le(far[1]))
+    V.wait_ge(T.sem.sqL, 2)
+    V.wait_ge(T.sem.sqP, 2)
+    e1, s1 = add(ll(r), ll(p))
+    V.wait_ge(s1, 1)
+    V.wait_ge(s2, 1)
+    te, ste = add(e1, e2)
+
+    def pre_late():
+        V.wait_ge(T.sem.sqE, 2)
+        V.wait_ge(T.sem.eaP, nin(p))
+        return add(le(r), le(p))
+    pre, spre = finish(te, ste, far, T.sem.yE, pre_late)
+
+    V.wait_ge(spre, 1)
+    V.wait_ge(T.sem["la%d" % far_o[0]], nin(far_o[0]))
+    p1, sp1 = add(pre, ll(far_o[0]))
+    V.wait_ge(sp1, 1)
+    V.wait_ge(T.sem["la%d" % far_o[1]], nin(far_o[1]))
+    tl, stl = add(p1, ll(far_o[1]))
+    finish(tl, stl, here, T.sem.yL)
+
+    def store(blocks, ysem, sem):
+        SY.wait_ge(ysem, 2)
+        runs = [(blocks[0], 2)] if blocks[1] == blocks[0] + 1 else [(blocks[0], 1), (blocks[1], 1)]
+        for lo, n in runs:
+            SY.dma_start(T.y[:, NC * lo:NC * (lo + n)], T.ysb[:, NC * lo:NC * (lo + n)]).then_inc(sem, 16)
+        return 16 * len(runs)
+    ne = store(far, T.sem.yE, T.sem.stE)
+    nl = store(here, T.sem.yL, T.sem.stL)
+    SY.wait_ge(T.sem.stE, ne)
+    SY.wait_ge(T.sem.stL, nl)

@@ -35,8 +35,7 @@ def _plan(topo, cores, s):
         return [e for e in range(m.bit_length()) if (m >> e) & 1]
     off = bits(topo.mask(c, cores[far[0]]))
     on = [e for e in bits(topo.mask(c, cores[p])) if e not in off]
-    h = len(off) // 2
-    return here, far, far_o, p, {far_o[0]: off[:h], far_o[1]: off[h:], p: on}
+    return here, far, far_o, p, off, on
 
 
 def rank_program(g, core, T, topo):
@@ -46,10 +45,8 @@ def rank_program(g, core, T, topo):
     cores = T.cores
     V, S, PE, SY = g.vector, g.scalar, g.tensor, g.sync
     A, F = AluOpType, ActivationFunctionType
-    here, far, far_o, p, eng = _plan(topo, cores, r)
-
-    def nin(s):
-        return len(_plan(topo, cores, s)[4][r])
+    here, far, far_o, p, off, on = _plan(topo, cores, r)
+    no, nn = len(off), len(on)
     sent = [0]
     nsem = [0]
 
@@ -57,13 +54,13 @@ def rank_program(g, core, T, topo):
         nsem[0] += 1
         return T.sem["c%d" % (nsem[0] - 1)]
 
-    def send(src, dst, dests):
+    def send(pieces):
         trs = []
-        for d, sem in dests:
+        for src, dst, d, engines, sem in pieces:
             rid, pid = topo.addr(cores[d], core)
-            trs.append(RemoteDMATransfer(dst_ids=[DstId(rid=rid, pnc=pid)], dma_engine_mask=sum(1 << e for e in eng[d]),
+            trs.append(RemoteDMATransfer(dst_ids=[DstId(rid=rid, pnc=pid)], dma_engine_mask=sum(1 << e for e in engines),
                                          remote_sem=sem, src=src, dst=dst))
-            sent[0] += len(eng[d])
+            sent[0] += len(engines)
         g.remote_dma_fused(trs, local_sem=T.sem.snt)
 
     def xcol(j):
@@ -76,9 +73,9 @@ def rank_program(g, core, T, topo):
         return T.ll[:, 4 * j:4 * j + 2]
     nslot = [0]
 
-    def slot():
+    def slot(n=2):
         nslot[0] += 1
-        return T.tmp[:, 4 * (nslot[0] - 1):4 * (nslot[0] - 1) + 2]
+        return T.tmp[:, 4 * (nslot[0] - 1):4 * (nslot[0] - 1) + n]
 
     SY.dma_start(T.xb[:], T.x[:]).then_inc(T.sem.ldx, 16)
     SY.dma_start(T.wb[:], T.w[:]).then_inc(T.sem.ldw, 16)
@@ -87,19 +84,26 @@ def rank_program(g, core, T, topo):
     V.wait_ge(T.sem.ldw, 16)
     V.quantize_mx(T.wq[:, 0:NC], T.ws[:, 0:NC], T.wb[:]).then_inc(T.sem.qw, 1)
 
-    others = [far_o[0], far_o[1], p]
     xa = T.sem["xa%d" % r]
-    g.wait_ge(T.sem.qx, 1)
+    f0, f1 = far_o
+    H = NC // 2
     cx = T.xq[:, xcol(r)].bitcast(dt.uint8)
-    send(cx, cx, [(d, xa) for d in others])
-    send(T.xs[:, xcol(r)], T.xs[:, xcol(r)], [(d, xa) for d in others])
+    px = T.xs[:, xcol(r)]
+    g.wait_ge(T.sem.qx, 1)
+    send([(cx, cx, f0, off, xa), (cx, cx, p, on, xa)])
+    send([(px, px, f0, off, xa), (px, px, p, on, xa)])
     g.wait_ge(T.sem.qw, 1)
-    send(T.wq[:, 0:NC].bitcast(dt.uint8), T.wq[:, NC:2 * NC].bitcast(dt.uint8), [(p, T.sem.wa)])
-    send(T.ws[:, 0:NC], T.ws[:, NC:2 * NC], [(p, T.sem.wa)])
+    send([(cx, cx, f1, off, xa)]
+         + [(T.wq[:, H * i:H * i + H].bitcast(dt.uint8), T.wq[:, NC + H * i:NC + H * i + H].bitcast(dt.uint8), p,
+             on[nn // 2 * i:nn // 2 * (i + 1)], T.sem.wa) for i in range(2)])
+    send([(px, px, f1, off, xa)]
+         + [(T.ws[:, H * i:H * i + H], T.ws[:, NC + H * i:NC + H * i + H], p,
+             on[nn // 2 * i:nn // 2 * (i + 1)], T.sem.wa) for i in range(2)])
+    oh = [off[:no // 2], off[no // 2:]]
     g.wait_ge(T.sem.sqE, 2)
-    send(le(r), le(r), [(far_o[0], T.sem.eaR), (far_o[1], T.sem.eaR), (p, T.sem.eaP)])
+    send([(le(r), le(r), f0, oh[0], T.sem.eaR), (le(r), le(r), f1, oh[1], T.sem.eaR), (le(r), le(r), p, on, T.sem.eaP)])
     g.wait_ge(T.sem.sqL, 2)
-    send(ll(r), ll(r), [(d, T.sem["la%d" % r]) for d in far_o])
+    send([(ll(r), ll(r), f0, oh[0], T.sem["la%d" % r]), (ll(r), ll(r), f1, oh[1], T.sem["la%d" % r])])
     g.wait_ge(T.sem.snt, sent[0])
 
     def mm(j, wlo, bank):
@@ -108,10 +112,12 @@ def rank_program(g, core, T, topo):
     PE.wait_ge(T.sem.qx, 1)
     PE.wait_ge(T.sem.qw, 1)
     mm(r, 0, r)
-    for j in [p] + far_o:
-        PE.wait_ge(T.sem["xa%d" % j], 2 * nin(j))
+    PE.wait_ge(T.sem["xa%d" % p], 2 * nn)
+    mm(p, 0, p)
+    for j in far_o:
+        PE.wait_ge(T.sem["xa%d" % j], 2 * no)
         mm(j, 0, j)
-    PE.wait_ge(T.sem.wa, 2 * nin(p))
+    PE.wait_ge(T.sem.wa, 2 * nn)
     for i, j in enumerate(far_o):
         mm(j, NC, N + i)
 
@@ -134,56 +140,58 @@ def rank_program(g, core, T, topo):
         V.tensor_tensor(o, a, b, A.add).then_inc(s, 1)
         return o, s
 
-    def finish(tot, s_tot, blocks, ysem, between=None):
-        q, v, u, a, b, t, rr = [slot() for _ in range(7)]
-        sq_, sv, su, sa, sb, st, sr = [new_sem() for _ in range(7)]
+    q, v, u, a4, b4, t4, rr = [slot(4) for _ in range(7)]
+
+    def root(tot, s_tot, lo):
+        sq_, sv = new_sem(), new_sem()
         S.wait_ge(s_tot, 1)
-        S.activation(q, tot, F.Sqrt, bias=EPS * 2.0 ** (-2 * K), scale=1.0 / (N * NC)).then_inc(sq_, 1)
+        S.activation(q[:, lo:lo + 2], tot, F.Sqrt, bias=EPS * 2.0 ** (-2 * K), scale=1.0 / (N * NC)).then_inc(sq_, 1)
         V.wait_ge(s_tot, 1)
-        V.tensor_scalar(v, tot, 2.0 ** K / (N * NC), EPS * 2.0 ** -K, A.mult, A.add).then_inc(sv, 1)
-        V.wait_ge(sv, 1)
-        V.reciprocal(u, v).then_inc(su, 1)
-        res = between() if between else None
-        V.wait_ge(su, 1)
-        V.wait_ge(sq_, 1)
-        V.tensor_tensor(a, q, u, A.mult).then_inc(sa, 1)
-        V.wait_ge(sa, 1)
-        V.tensor_tensor(b, a, q, A.mult).then_inc(sb, 1)
-        V.wait_ge(sb, 1)
-        V.tensor_scalar(t, b, -0.5 * 2.0 ** K, 1.5, A.mult, A.add).then_inc(st, 1)
-        V.wait_ge(st, 1)
-        V.tensor_tensor(rr, a, t, A.mult).then_inc(sr, 1)
-        V.wait_ge(sr, 1)
-        S.wait_ge(sr, 1)
+        V.tensor_scalar(v[:, lo:lo + 2], tot, 2.0 ** K / (N * NC), EPS * 2.0 ** -K, A.mult, A.add).then_inc(sv, 1)
+        return sq_, sv
+
+    V.wait_ge(T.sem.sqE, 2)
+    V.wait_ge(T.sem.eaP, nn)
+    pre, spre = add(le(r), le(p))
+    V.wait_ge(T.sem.eaR, no)
+    e2, s2 = add(le(far[0]), le(far[1]))
+    V.wait_ge(s2, 1)
+    V.wait_ge(T.sem.sqL, 2)
+    e1, s1 = add(e2, ll(r))
+    V.wait_ge(s1, 1)
+    V.wait_ge(T.sem.sqP, 2)
+    te, ste = add(e1, ll(p))
+    sqF, svF = root(te, ste, 0)
+    V.wait_ge(spre, 1)
+    V.wait_ge(T.sem["la%d" % f0], no // 2)
+    p1, sp1 = add(pre, ll(f0))
+    V.wait_ge(sp1, 1)
+    V.wait_ge(T.sem["la%d" % f1], no // 2)
+    tl, stl = add(p1, ll(f1))
+    sqL_, svL = root(tl, stl, 2)
+
+    su, sa, sb, st, sr = [new_sem() for _ in range(5)]
+    V.wait_ge(svF, 1)
+    V.wait_ge(svL, 1)
+    V.reciprocal(u, v).then_inc(su, 1)
+    V.wait_ge(su, 1)
+    V.wait_ge(sqF, 1)
+    V.wait_ge(sqL_, 1)
+    V.tensor_tensor(a4, q, u, A.mult).then_inc(sa, 1)
+    V.wait_ge(sa, 1)
+    V.tensor_tensor(b4, a4, q, A.mult).then_inc(sb, 1)
+    V.wait_ge(sb, 1)
+    V.tensor_scalar(t4, b4, -0.5 * 2.0 ** K, 1.5, A.mult, A.add).then_inc(st, 1)
+    V.wait_ge(st, 1)
+    V.tensor_tensor(rr, a4, t4, A.mult).then_inc(sr, 1)
+    V.wait_ge(sr, 1)
+    S.wait_ge(sr, 1)
+    for blocks, lo, ysem in ((far, 0, T.sem.yE), (here, 2, T.sem.yL)):
         j0, j1 = blocks
-        V.tensor_scalar(T.ysb[:, NC * j0:NC * j0 + NC], T.z[:, 512 * j0:512 * j0 + NC], rr[:, 0:1], None,
+        V.tensor_scalar(T.ysb[:, NC * j0:NC * j0 + NC], T.z[:, 512 * j0:512 * j0 + NC], rr[:, lo:lo + 1], None,
                         A.mult).then_inc(ysem, 1)
         S.activation(T.ysb[:, NC * j1:NC * j1 + NC], T.z[:, 512 * j1:512 * j1 + NC], F.Copy,
-                     scale=rr[:, 1:2]).then_inc(ysem, 1)
-        return res
-
-    V.wait_ge(T.sem.eaR, nin(far[0]) + nin(far[1]))
-    e2, s2 = add(le(far[0]), le(far[1]))
-    V.wait_ge(T.sem.sqL, 2)
-    V.wait_ge(T.sem.sqP, 2)
-    e1, s1 = add(ll(r), ll(p))
-    V.wait_ge(s1, 1)
-    V.wait_ge(s2, 1)
-    te, ste = add(e1, e2)
-
-    def pre_late():
-        V.wait_ge(T.sem.sqE, 2)
-        V.wait_ge(T.sem.eaP, nin(p))
-        return add(le(r), le(p))
-    pre, spre = finish(te, ste, far, T.sem.yE, pre_late)
-
-    V.wait_ge(spre, 1)
-    V.wait_ge(T.sem["la%d" % far_o[0]], nin(far_o[0]))
-    p1, sp1 = add(pre, ll(far_o[0]))
-    V.wait_ge(sp1, 1)
-    V.wait_ge(T.sem["la%d" % far_o[1]], nin(far_o[1]))
-    tl, stl = add(p1, ll(far_o[1]))
-    finish(tl, stl, here, T.sem.yL)
+                     scale=rr[:, lo + 1:lo + 2]).then_inc(ysem, 1)
 
     def store(blocks, ysem, sem):
         SY.wait_ge(ysem, 2)

from concourse.bass import DstId, RemoteDMATransfer
from concourse.mybir import dt, AluOpType, ActivationFunctionType

N, NC, TK, EPS = 4, 256, 128, 0.001
K = 20
NCHAIN = 32

SCRATCH = {
    "xb": ("sbuf", [128, 4 * TK], "bfloat16"),
    "wb": ("sbuf", [128, 4 * NC], "bfloat16"),
    "xq": ("sbuf", [128, N * TK], "float8_e4m3fn_x4"),
    "xs": ("sbuf", [128, N * TK], "uint8"),
    "wq": ("sbuf", [128, 2 * NC], "float8_e4m3fn_x4"),
    "ws": ("sbuf", [128, 2 * NC], "uint8"),
    "z": ("psum", [128, 512 * 6], "float32"),
    "sq": ("sbuf", [128, 6 * NC], "float32"),
    "le": ("sbuf", [128, 4 * N], "float32"),
    "ll": ("sbuf", [128, 4 * N], "float32"),
    "tmp": ("sbuf", [128, 4 * 28], "float32"),
    "ysb": ("sbuf", [128, N * NC], "float32"),
}
SEMAPHORES = (["ldx", "ldw", "qx", "qw", "wa", "sqE", "sqL", "sqP", "eaP", "eaR", "snt", "yE", "yL", "stE", "stL"]
              + ["xa%d" % j for j in range(N)] + ["la%d" % j for j in range(N)] + ["mm%d" % j for j in range(6)]
              + ["c%d" % j for j in range(NCHAIN)])


def _plan(topo, cores, s):
    c = cores[s]
    here = [j for j in range(N) if topo.host(cores[j]) == topo.host(c) and topo.chip(cores[j]) == topo.chip(c)]
    far = [j for j in range(N) if j not in here]
    far_o = sorted(far, key=lambda j: (topo.die(cores[j]) != topo.die(c), j))
    p = [j for j in here if j != s][0]

    def bits(m):
        return [e for e in range(m.bit_length()) if (m >> e) & 1]
    off = bits(topo.mask(c, cores[far[0]]))
    on = [e for e in bits(topo.mask(c, cores[p])) if e not in off]
    return here, far, far_o, p, off, on


def rank_program(g, core, T, topo):
    r = T.rank_of(core)
    if r is None:
        return
    cores = T.cores
    V, S, PE, SY = g.vector, g.scalar, g.tensor, g.sync
    A, F = AluOpType, ActivationFunctionType
    here, far, far_o, p, off, on = _plan(topo, cores, r)
    no, nn = len(off), len(on)
    sent = [0]
    nsem = [0]

    def new_sem():
        nsem[0] += 1
        return T.sem["c%d" % (nsem[0] - 1)]

    def send(pieces):
        trs = []
        for src, dst, d, engines, sem in pieces:
            rid, pid = topo.addr(cores[d], core)
            trs.append(RemoteDMATransfer(dst_ids=[DstId(rid=rid, pnc=pid)], dma_engine_mask=sum(1 << e for e in engines),
                                         remote_sem=sem, src=src, dst=dst))
            sent[0] += len(engines)
        g.remote_dma_fused(trs, local_sem=T.sem.snt)

    def xcol(j):
        return slice(TK * j, TK * j + TK)

    def le(j):
        return T.le[:, 4 * j:4 * j + 2]

    def ll(j):
        return T.ll[:, 4 * j:4 * j + 2]
    nslot = [0]

    def slot(n=2):
        nslot[0] += 1
        return T.tmp[:, 4 * (nslot[0] - 1):4 * (nslot[0] - 1) + n]

    SY.dma_start(T.xb[:], T.x[:]).then_inc(T.sem.ldx, 16)
    SY.dma_start(T.wb[:], T.w[:]).then_inc(T.sem.ldw, 16)
    V.wait_ge(T.sem.ldx, 16)
    V.quantize_mx(T.xq[:, xcol(r)], T.xs[:, xcol(r)], T.xb[:]).then_inc(T.sem.qx, 1)
    V.wait_ge(T.sem.ldw, 16)
    V.quantize_mx(T.wq[:, 0:NC], T.ws[:, 0:NC], T.wb[:]).then_inc(T.sem.qw, 1)

    xa = T.sem["xa%d" % r]
    f0, f1 = far_o
    H = NC // 2
    cx = T.xq[:, xcol(r)].bitcast(dt.uint8)
    px = T.xs[:, xcol(r)]
    g.wait_ge(T.sem.qx, 1)
    send([(cx, cx, f0, off, xa), (cx, cx, p, on, xa)])
    send([(px, px, f0, off, xa), (px, px, p, on, xa)])
    g.wait_ge(T.sem.qw, 1)
    send([(cx, cx, f1, off, xa)]
         + [(T.wq[:, H * i:H * i + H].bitcast(dt.uint8), T.wq[:, NC + H * i:NC + H * i + H].bitcast(dt.uint8), p,
             on[nn // 2 * i:nn // 2 * (i + 1)], T.sem.wa) for i in range(2)])
    send([(px, px, f1, off, xa)]
         + [(T.ws[:, H * i:H * i + H], T.ws[:, NC + H * i:NC + H * i + H], p,
             on[nn // 2 * i:nn // 2 * (i + 1)], T.sem.wa) for i in range(2)])
    oh = [off[:no // 2], off[no // 2:]]
    g.wait_ge(T.sem.sqE, 2)
    send([(le(r), le(r), f0, oh[0], T.sem.eaR), (le(r), le(r), f1, oh[1], T.sem.eaR), (le(r), le(r), p, on, T.sem.eaP)])
    g.wait_ge(T.sem.sqL, 2)
    send([(ll(r), ll(r), f0, oh[0], T.sem["la%d" % r]), (ll(r), ll(r), f1, oh[1], T.sem["la%d" % r])])
    g.wait_ge(T.sem.snt, sent[0])

    def mm(j, wlo, bank):
        PE.matmul_mx(T.z[:, 512 * bank:512 * bank + NC], T.xq[:, xcol(j)], T.xs[:, xcol(j)],
                     T.wq[:, wlo:wlo + NC], T.ws[:, wlo:wlo + NC], True, True).then_inc(T.sem["mm%d" % bank], 1)
    PE.wait_ge(T.sem.qx, 1)
    PE.wait_ge(T.sem.qw, 1)
    mm(r, 0, r)
    PE.wait_ge(T.sem["xa%d" % p], 2 * nn)
    mm(p, 0, p)
    for j in far_o:
        PE.wait_ge(T.sem["xa%d" % j], 2 * no)
        mm(j, 0, j)
    PE.wait_ge(T.sem.wa, 2 * nn)
    for i, j in enumerate(far_o):
        mm(j, NC, N + i)

    def square(bank, acc, sem):
        S.wait_ge(T.sem["mm%d" % bank], 1)
        S.activation(T.sq[:, NC * bank:NC * bank + NC], T.z[:, 512 * bank:512 * bank + NC], F.Square,
                     scale=2.0 ** -K, accum_out=acc).then_inc(sem, 1)
    for j in [r, p]:
        c = 4 * r + here.index(j)
        square(j, T.le[:, c:c + 1], T.sem.sqE)
    for j in far_o:
        c = 4 * r + far.index(j)
        square(j, T.ll[:, c:c + 1], T.sem.sqL)
    for i, j in enumerate(far_o):
        c = 4 * p + far.index(j)
        square(N + i, T.ll[:, c:c + 1], T.sem.sqP)

    def add(a, b):
        o, s = slot(), new_sem()
        V.tensor_tensor(o, a, b, A.add).then_inc(s, 1)
        return o, s

    q, v, u, a4, b4, t4, rr = [slot(4) for _ in range(7)]

    def root(tot, s_tot, lo):
        sq_, sv = new_sem(), new_sem()
        S.wait_ge(s_tot, 1)
        S.activation(q[:, lo:lo + 2], tot, F.Sqrt, bias=EPS * 2.0 ** (-2 * K), scale=1.0 / (N * NC)).then_inc(sq_, 1)
        V.wait_ge(s_tot, 1)
        V.tensor_scalar(v[:, lo:lo + 2], tot, 2.0 ** K / (N * NC), EPS * 2.0 ** -K, A.mult, A.add).then_inc(sv, 1)
        return sq_, sv

    V.wait_ge(T.sem.sqE, 2)
    V.wait_ge(T.sem.eaP, nn)
    pre, spre = add(le(r), le(p))
    V.wait_ge(T.sem.eaR, no)
    e2, s2 = add(le(far[0]), le(far[1]))
    V.wait_ge(s2, 1)
    V.wait_ge(T.sem.sqL, 2)
    e1, s1 = add(e2, ll(r))
    V.wait_ge(s1, 1)
    V.wait_ge(T.sem.sqP, 2)
    te, ste = add(e1, ll(p))
    sqF, svF = root(te, ste, 0)
    V.wait_ge(spre, 1)
    V.wait_ge(T.sem["la%d" % f0], no // 2)
    p1, sp1 = add(pre, ll(f0))
    V.wait_ge(sp1, 1)
    V.wait_ge(T.sem["la%d" % f1], no // 2)
    tl, stl = add(p1, ll(f1))
    sqL_, svL = root(tl, stl, 2)

    su, sa, sb, st, sr = [new_sem() for _ in range(5)]
    V.wait_ge(svF, 1)
    V.wait_ge(svL, 1)
    V.reciprocal(u, v).then_inc(su, 1)
    V.wait_ge(su, 1)
    V.wait_ge(sqF, 1)
    V.wait_ge(sqL_, 1)
    V.tensor_tensor(a4, q, u, A.mult).then_inc(sa, 1)
    V.wait_ge(sa, 1)
    V.tensor_tensor(b4, a4, q, A.mult).then_inc(sb, 1)
    V.wait_ge(sb, 1)
    V.tensor_scalar(t4, b4, -0.5 * 2.0 ** K, 1.5, A.mult, A.add).then_inc(st, 1)
    V.wait_ge(st, 1)
    V.tensor_tensor(rr, a4, t4, A.mult).then_inc(sr, 1)
    V.wait_ge(sr, 1)
    S.wait_ge(sr, 1)
    for blocks, lo, ysem in ((far, 0, T.sem.yE), (here, 2, T.sem.yL)):
        j0, j1 = blocks
        V.tensor_scalar(T.ysb[:, NC * j0:NC * j0 + NC], T.z[:, 512 * j0:512 * j0 + NC], rr[:, lo:lo + 1], None,
                        A.mult).then_inc(ysem, 1)
        S.activation(T.ysb[:, NC * j1:NC * j1 + NC], T.z[:, 512 * j1:512 * j1 + NC], F.Copy,
                     scale=rr[:, lo + 1:lo + 2]).then_inc(ysem, 1)

    def store(blocks, ysem, sem):
        SY.wait_ge(ysem, 2)
        runs = [(blocks[0], 2)] if blocks[1] == blocks[0] + 1 else [(blocks[0], 1), (blocks[1], 1)]
        for lo, n in runs:
            SY.dma_start(T.y[:, NC * lo:NC * (lo + n)], T.ysb[:, NC * lo:NC * (lo + n)]).then_inc(sem, 16)
        return 16 * len(runs)
    ne = store(far, T.sem.yE, T.sem.stE)
    nl = store(here, T.sem.yL, T.sem.stL)
    SY.wait_ge(T.sem.stE, ne)
    SY.wait_ge(T.sem.stL, nl)
